import numpy as np
import ml_dtypes


def mxq(x, axis, fmt="e4m3"):
    dtype, down = {"e4m3": (ml_dtypes.float8_e4m3fn, 7), "e5m2": (ml_dtypes.float8_e5m2, 14)}[fmt]
    v = np.moveaxis(np.asarray(x, np.float32).astype(ml_dtypes.bfloat16).astype(np.float64), axis, -1)
    blocks = v.reshape(v.shape[:-1] + (-1, 32))
    amax = np.abs(blocks).max(-1, keepdims=True)
    byte = np.maximum(np.where(amax > 0, np.frexp(amax)[1] - 1 + 127, 0) - down, 1)
    scale = np.exp2(byte - 127.0)
    codes = (blocks / scale).astype(np.float32).astype(dtype).astype(np.float64)
    return np.moveaxis((codes * scale).reshape(v.shape), -1, axis)


WIDE = False


def mx_kscale(k):
    if not WIDE:
        return np.ones(k)
    levels = np.array([10, -10, 5, -5, 0])
    if k % 512:
        return np.exp2(np.random.permutation(np.resize(levels, k // 32))).repeat(32)
    a = np.empty((k // 512, 16))
    for p in range(k // 512):
        a[p, :8] = np.random.permutation(np.resize(levels, 8))
        for g in range(8):
            far = levels[np.abs(levels - a[p, g]) >= 10]
            a[p, g + 8] = far[np.random.randint(len(far))]
    return np.exp2(a.ravel()).repeat(32)


def f64(x):
    return np.asarray(x).astype(np.float64)


def striped(idx):
    return np.tile(idx.reshape(-1, 16).T, (8, 1)).astype(np.uint16)


def unstriped(offs):
    return offs[:16].T.reshape(-1).astype(np.int64)


E2M1 = np.array([0.0, 0.5, 1.0, 1.5, 2.0, 3.0, 4.0, 6.0, -0.0, -0.5, -1.0, -1.5, -2.0, -3.0, -4.0, -6.0])


def pack_fp4(w):
    k, n = w.shape
    w = f64(np.asarray(w, np.float32).astype(ml_dtypes.bfloat16)).reshape(k // 32, 32, n)
    amax = np.abs(w).max(1)
    mant, ex = np.frexp(amax / 6.0)
    byte = np.clip(np.where(amax > 0, np.where(mant > 0.5, ex, ex - 1) + 127, 1), 1, 254)
    scaled = (w * np.exp2(127.0 - byte)[:, None, :]).reshape(k, n).astype(np.float32)
    c = np.ascontiguousarray(scaled.reshape(k // 512, 128, 4, n).transpose(0, 1, 3, 2)).astype(ml_dtypes.float4_e2m1fn).view(np.uint8) & 0xF
    words = (c[..., 0::2] | (c[..., 1::2] << 4)).reshape(k // 512, 128, 2 * n)
    return np.ascontiguousarray(words), np.ascontiguousarray(byte.astype(np.uint8).reshape(k // 512, 16, n))


def unpack_fp4(words, scales):
    g, _, n = scales.shape
    words = np.ascontiguousarray(words).reshape(g, 128, n, 2)
    nib = np.empty((g, 128, n, 4), np.uint8)
    nib[..., 0::2] = words & 0xF
    nib[..., 1::2] = words >> 4
    vals = E2M1[nib] * np.repeat(np.exp2(scales.astype(np.float64) - 127.0), 8, axis=1)[..., None]
    return vals.transpose(0, 1, 3, 2).reshape(g * 512, n)


def gelu(v):
    return 0.5 * v * (1.0 + np.tanh(np.sqrt(2.0 / np.pi) * (v + 0.044715 * v**3)))


K, T, N, U = 1024, 1024, 128, 2048
P = 2 ** 7


def setup_inputs():
    n = np.random.standard_normal
    s = mx_kscale(K)[:, None]
    packed_xT = pack_fp4(n((K, T)) * s)
    return {
        "x_words": packed_xT[0],
        "x_scales": packed_xT[1],
        "gate": np.tile(np.random.uniform(0.5, 1.5, T), (P, 1)).astype(np.float32),
        "w1": (n((K, N)) / np.sqrt(K) / s).astype(np.float32),
        "dst": striped(np.random.permutation(U)[:T]),
    }


def reference(x_words, x_scales, gate, w1, dst):
    xq = unpack_fp4(x_words, x_scales)
    y = gelu(mxq(f64(w1), 0, "e4m3").T @ xq)
    out = np.zeros((N, U))
    out[:, unstriped(dst)] = y * f64(gate)[:1]
    return out

@@ -1,0 +1,97 @@
+from contextlib import ExitStack
+
+import concourse.mybir as mybir
+
+K, T, N, U = 1024, 1024, 128, 2048
+FLOPS = 2 * K * T * N
+
+F32 = mybir.dt.float32
+BF16 = mybir.dt.bfloat16
+I32 = mybir.dt.int32
+U32 = mybir.dt.uint32
+U16 = mybir.dt.uint16
+U8 = mybir.dt.uint8
+FP8X4 = mybir.dt.float8_e4m3fn_x4
+FP4X4 = mybir.dt.float4_e2m1fn_x4
+GELU = mybir.ActivationFunctionType.Gelu_apprx_tanh
+MULT = mybir.AluOpType.mult
+
+P = 128
+PACK = 4
+K_PASS = P * PACK
+PASSES = K // K_PASS
+HALF = T // 2
+PIECES = ((128, 128), (128, 128), (512,))
+
+
+def tile_picked_wroute2_lingelu_l_kernel(tc, x_words, x_scales, gate, w1, dst, out):
+    nc = tc.nc
+    with ExitStack() as ctx:
+        keep = ctx.enter_context(tc.tile_pool(name="keep", bufs=1))
+        psum = ctx.enter_context(tc.psum_pool(name="psum", bufs=1))
+
+        offsets = keep.tile([P, T // 16], U16, name="offsets")
+        x_scale = keep.tile([P, PASSES, T], U8, name="x_scale", align_bytes=64)
+        window = keep.tile([P, U], F32, name="window")
+        nc.vector.memset(x_scale[:].bitcast(I32), 0)
+        nc.vector.memset(window[:], 0.0)
+
+        w_raw = [keep.tile([P, PACK, N], F32, name="w_raw%d" % g) for g in range(PASSES)]
+        for g in range(PASSES):
+            nc.sync.dma_start(out=w_raw[g][:], in_=w1[g * K_PASS:(g + 1) * K_PASS, :].rearrange("(p j) m -> p j m", j=PACK))
+        for q in range(4):
+            nc.sync.dma_start(
+                out=x_scale[32 * q:32 * q + 4, :, :].bitcast(I32),
+                in_=x_scales[:, 4 * q:4 * q + 4, :].rearrange("z r c -> r z c").bitcast(I32),
+            )
+        x_code = [keep.tile([P, PASSES, 2 * HALF], U8, name="x_code%d" % h, align_bytes=64) for h in range(2)]
+        gates = [keep.tile([P, HALF], F32, name="gates%d" % h) for h in range(2)]
+        for h in range(2):
+            nc.sync.dma_start(
+                out=x_code[h][:].bitcast(I32),
+                in_=x_words[:, :, 2 * h * HALF:2 * (h + 1) * HALF].rearrange("z p b -> p z b").bitcast(I32),
+            )
+            if h == 0:
+                nc.sync.dma_start(offsets[:], dst)
+            nc.sync.dma_start(out=gates[h][:], in_=gate[:, h * HALF:(h + 1) * HALF])
+
+        w_code = []
+        w_scale = []
+        for g in range(PASSES):
+            grouped = keep.tile([P, N, PACK], BF16, name="grouped%d" % g, align_bytes=64)
+            nc.vector.tensor_copy(
+                out=grouped[:].rearrange("p (c i) t -> p c t i", i=4),
+                in_=w_raw[g][:].rearrange("p t (c i) -> p c t i", i=4),
+            )
+            codes = keep.tile([P, N], U32, name="w_code%d" % g, align_bytes=64)
+            scales = keep.tile([P, N], U8, name="w_scale%d" % g, align_bytes=64)
+            nc.vector.quantize_mx(out=codes[:].bitcast(FP8X4), scales=scales[:], in_=grouped[:].rearrange("p m t -> p (m t)"))
+            w_code.append(codes)
+            w_scale.append(scales)
+
+        t0 = 0
+        for i, widths in enumerate(PIECES):
+            n = sum(widths)
+            y = keep.tile([P, n], F32, name="y%d" % i)
+            h, c0 = divmod(t0, HALF)
+            a = 0
+            for width in widths:
+                acc = psum.tile([P, width], F32, name="acc%d" % (t0 + a))
+                for g in range(PASSES):
+                    nc.tensor.matmul_mx(
+                        out=acc[:],
+                        lhsT=w_code[g][:].bitcast(FP8X4),
+                        lhsT_scale=w_scale[g][:],
+                        rhs=x_code[h][:, g, 2 * (c0 + a):2 * (c0 + a + width)].bitcast(FP4X4),
+                        rhs_scale=x_scale[:, g, t0 + a:t0 + a + width],
+                        start=(g == 0),
+                        stop=(g == PASSES - 1),
+                    )
+                nc.scalar.activation(out=y[:, a:a + width], in_=acc[:], func=GELU)
+                a = a + width
+            nc.vector.tensor_tensor(
+                window[:].indirect(offsets[:, t0 // 16:(t0 + n) // 16]), y[:], gates[h][:, c0:c0 + n], MULT
+            )
+            t0 = t0 + n
+
+        nc.sync.dma_start(out=out, in_=window[:])

@@ -20,8 +20,7 @@ P = 128
 PACK = 4
 K_PASS = P * PACK
 PASSES = K // K_PASS
-HALF = T // 2
-PIECES = ((128, 128), (128, 128), (512,))
+PIECES = ((128, 128), (512, 128, 128))
 
 
 def tile_picked_wroute2_lingelu_l_kernel(tc, x_words, x_scales, gate, w1, dst, out):
@@ -33,39 +32,57 @@ def tile_picked_wroute2_lingelu_l_kernel(tc, x_words, x_scales, gate, w1, dst, o
         offsets = keep.tile([P, T // 16], U16, name="offsets")
         x_scale = keep.tile([P, PASSES, T], U8, name="x_scale", align_bytes=64)
         window = keep.tile([P, U], F32, name="window")
-        nc.vector.memset(x_scale[:].bitcast(I32), 0)
         nc.vector.memset(window[:], 0.0)
 
+        starts = [sum(sum(w) for w in PIECES[:i]) for i in range(len(PIECES) + 1)]
         w_raw = [keep.tile([P, PACK, N], F32, name="w_raw%d" % g) for g in range(PASSES)]
-        for g in range(PASSES):
+        x_code = [keep.tile([P, PASSES, 2 * sum(w)], U8, name="x_code%d" % i, align_bytes=64) for i, w in enumerate(PIECES)]
+        gates = [keep.tile([P, sum(w)], F32, name="gate%d" % i) for i, w in enumerate(PIECES)]
+
+        def load_weights(g):
             nc.sync.dma_start(out=w_raw[g][:], in_=w1[g * K_PASS:(g + 1) * K_PASS, :].rearrange("(p j) m -> p j m", j=PACK))
-        for q in range(4):
+
+        def load_codes(i):
             nc.sync.dma_start(
+                out=x_code[i][:].bitcast(I32),
+                in_=x_words[:, :, 2 * starts[i]:2 * starts[i + 1]].rearrange("z p b -> p z b").bitcast(I32),
+            )
+
+        def load_scales(engine, q):
+            engine.dma_start(
                 out=x_scale[32 * q:32 * q + 4, :, :].bitcast(I32),
                 in_=x_scales[:, 4 * q:4 * q + 4, :].rearrange("z r c -> r z c").bitcast(I32),
             )
-        x_code = [keep.tile([P, PASSES, 2 * HALF], U8, name="x_code%d" % h, align_bytes=64) for h in range(2)]
-        gates = [keep.tile([P, HALF], F32, name="gates%d" % h) for h in range(2)]
-        for h in range(2):
-            nc.sync.dma_start(
-                out=x_code[h][:].bitcast(I32),
-                in_=x_words[:, :, 2 * h * HALF:2 * (h + 1) * HALF].rearrange("z p b -> p z b").bitcast(I32),
-            )
-            if h == 0:
-                nc.sync.dma_start(offsets[:], dst)
-            nc.sync.dma_start(out=gates[h][:], in_=gate[:, h * HALF:(h + 1) * HALF])
+
+        def load_gate(i):
+            nc.sync.dma_start(out=gates[i][:], in_=gate[:, starts[i]:starts[i + 1]])
+
+        load_weights(0)
+        load_weights(1)
+        load_codes(0)
+        for q in range(4):
+            load_scales(nc.sync, q)
+        load_codes(1)
+        load_gate(0)
+        nc.sync.dma_start(offsets[:], dst)
+        load_gate(1)
 
         w_code = []
         w_scale = []
         for g in range(PASSES):
             grouped = keep.tile([P, N, PACK], BF16, name="grouped%d" % g, align_bytes=64)
-            nc.vector.tensor_copy(
-                out=grouped[:].rearrange("p (c i) t -> p c t i", i=4),
-                in_=w_raw[g][:].rearrange("p t (c i) -> p c t i", i=4),
-            )
             codes = keep.tile([P, N], U32, name="w_code%d" % g, align_bytes=64)
             scales = keep.tile([P, N], U8, name="w_scale%d" % g, align_bytes=64)
-            nc.vector.quantize_mx(out=codes[:].bitcast(FP8X4), scales=scales[:], in_=grouped[:].rearrange("p m t -> p (m t)"))
+            halves = [slice(0, N // 2), slice(N // 2, N)]
+            for cols in halves:
+                nc.vector.tensor_copy(
+                    out=grouped[:, cols, :].rearrange("p (c i) t -> p c t i", i=4),
+                    in_=w_raw[g][:, :, cols].rearrange("p t (c i) -> p c t i", i=4),
+                )
+            for cols in halves:
+                nc.vector.quantize_mx(
+                    out=codes[:, cols].bitcast(FP8X4), scales=scales[:, cols], in_=grouped[:, cols, :].rearrange("p m t -> p (m t)")
+                )
             w_code.append(codes)
             w_scale.append(scales)
 
@@ -73,7 +90,6 @@ def tile_picked_wroute2_lingelu_l_kernel(tc, x_words, x_scales, gate, w1, dst, o
         for i, widths in enumerate(PIECES):
             n = sum(widths)
             y = keep.tile([P, n], F32, name="y%d" % i)
-            h, c0 = divmod(t0, HALF)
             a = 0
             for width in widths:
                 acc = psum.tile([P, width], F32, name="acc%d" % (t0 + a))
@@ -82,7 +98,7 @@ def tile_picked_wroute2_lingelu_l_kernel(tc, x_words, x_scales, gate, w1, dst, o
                         out=acc[:],
                         lhsT=w_code[g][:].bitcast(FP8X4),
                         lhsT_scale=w_scale[g][:],
-                        rhs=x_code[h][:, g, 2 * (c0 + a):2 * (c0 + a + width)].bitcast(FP4X4),
+                        rhs=x_code[i][:, g, 2 * a:2 * (a + width)].bitcast(FP4X4),
                         rhs_scale=x_scale[:, g, t0 + a:t0 + a + width],
                         start=(g == 0),
                         stop=(g == PASSES - 1),
@@ -90,8 +106,9 @@ def tile_picked_wroute2_lingelu_l_kernel(tc, x_words, x_scales, gate, w1, dst, o
                 nc.scalar.activation(out=y[:, a:a + width], in_=acc[:], func=GELU)
                 a = a + width
             nc.vector.tensor_tensor(
-                window[:].indirect(offsets[:, t0 // 16:(t0 + n) // 16]), y[:], gates[h][:, c0:c0 + n], MULT
+                window[:].indirect(offsets[:, t0 // 16:(t0 + n) // 16]), y[:], gates[i][:], MULT
             )
             t0 = t0 + n
 
-        nc.sync.dma_start(out=out, in_=window[:])
+        nc.sync.dma_start(out=out[:, 0:U // 2], in_=window[:, 0:U // 2])
+        nc.scalar.dma_start(out=out[:, U // 2:U], in_=window[:, U // 2:U])

@@ -110,5 +110,4 @@ def tile_picked_wroute2_lingelu_l_kernel(tc, x_words, x_scales, gate, w1, dst, o
             )
             t0 = t0 + n
 
-        nc.sync.dma_start(out=out[:, 0:U // 2], in_=window[:, 0:U // 2])
-        nc.scalar.dma_start(out=out[:, U // 2:U], in_=window[:, U // 2:U])
+        nc.sync.dma_start(out=out, in_=window[:])

@@ -20,7 +20,10 @@ P = 128
 PACK = 4
 K_PASS = P * PACK
 PASSES = K // K_PASS
-PIECES = ((128, 128), (512, 128, 128))
+GROUP = 128
+FIRST = 256
+WORD_LOADS = ((0, 256), (256, 1024))
+GROUPS = ((128, 128), (128,) * 6)
 
 
 def tile_picked_wroute2_lingelu_l_kernel(tc, x_words, x_scales, gate, w1, dst, out):
@@ -30,42 +33,49 @@ def tile_picked_wroute2_lingelu_l_kernel(tc, x_words, x_scales, gate, w1, dst, o
         psum = ctx.enter_context(tc.psum_pool(name="psum", bufs=1))
 
         offsets = keep.tile([P, T // 16], U16, name="offsets")
-        x_scale = keep.tile([P, PASSES, T], U8, name="x_scale", align_bytes=64)
         window = keep.tile([P, U], F32, name="window")
         nc.vector.memset(window[:], 0.0)
 
-        starts = [sum(sum(w) for w in PIECES[:i]) for i in range(len(PIECES) + 1)]
+        pieces = ((0, FIRST), (FIRST, T))
         w_raw = [keep.tile([P, PACK, N], F32, name="w_raw%d" % g) for g in range(PASSES)]
-        x_code = [keep.tile([P, PASSES, 2 * sum(w)], U8, name="x_code%d" % i, align_bytes=64) for i, w in enumerate(PIECES)]
-        gates = [keep.tile([P, sum(w)], F32, name="gate%d" % i) for i, w in enumerate(PIECES)]
+        x_code = [keep.tile([P, PASSES, 2 * (b - a)], U8, name="x_code%d" % a, align_bytes=64) for a, b in WORD_LOADS]
+        x_scale = keep.tile([P, PASSES, T], U8, name="x_scale", align_bytes=64)
+        gates = [keep.tile([P, b - a], F32, name="gate%d" % a) for a, b in pieces]
 
         def load_weights(g):
             nc.sync.dma_start(out=w_raw[g][:], in_=w1[g * K_PASS:(g + 1) * K_PASS, :].rearrange("(p j) m -> p j m", j=PACK))
 
         def load_codes(i):
+            a, b = WORD_LOADS[i]
             nc.sync.dma_start(
                 out=x_code[i][:].bitcast(I32),
-                in_=x_words[:, :, 2 * starts[i]:2 * starts[i + 1]].rearrange("z p b -> p z b").bitcast(I32),
+                in_=x_words[:, :, 2 * a:2 * b].rearrange("z p b -> p z b").bitcast(I32),
             )
 
-        def load_scales(engine, q):
+        def load_scales(engine, r):
             engine.dma_start(
-                out=x_scale[32 * q:32 * q + 4, :, :].bitcast(I32),
-                in_=x_scales[:, 4 * q:4 * q + 4, :].rearrange("z r c -> r z c").bitcast(I32),
+                out=x_scale[r:P:32, :, :].bitcast(I32),
+                in_=x_scales[:, r:16:4, :].rearrange("z q c -> q z c").bitcast(I32),
             )
 
-        def load_gate(i):
-            nc.sync.dma_start(out=gates[i][:], in_=gate[:, starts[i]:starts[i + 1]])
+        def load_gate(engine, i):
+            a, b = pieces[i]
+            engine.dma_start(out=gates[i][:], in_=gate[:, a:b])
 
+        def load_list():
+            nc.sync.dma_start(offsets[:], dst)
+
+        load_scales(nc.scalar, 0)
         load_weights(0)
         load_weights(1)
         load_codes(0)
-        for q in range(4):
-            load_scales(nc.sync, q)
+        load_scales(nc.sync, 1)
+        load_scales(nc.sync, 2)
+        load_scales(nc.sync, 3)
         load_codes(1)
-        load_gate(0)
-        nc.sync.dma_start(offsets[:], dst)
-        load_gate(1)
+        load_gate(nc.sync, 0)
+        load_list()
+        load_gate(nc.sync, 1)
 
         w_code = []
         w_scale = []
@@ -86,28 +96,31 @@ def tile_picked_wroute2_lingelu_l_kernel(tc, x_words, x_scales, gate, w1, dst, o
             w_code.append(codes)
             w_scale.append(scales)
 
-        t0 = 0
-        for i, widths in enumerate(PIECES):
-            n = sum(widths)
-            y = keep.tile([P, n], F32, name="y%d" % i)
-            a = 0
-            for width in widths:
-                acc = psum.tile([P, width], F32, name="acc%d" % (t0 + a))
-                for g in range(PASSES):
-                    nc.tensor.matmul_mx(
-                        out=acc[:],
-                        lhsT=w_code[g][:].bitcast(FP8X4),
-                        lhsT_scale=w_scale[g][:],
-                        rhs=x_code[i][:, g, 2 * a:2 * (a + width)].bitcast(FP4X4),
-                        rhs_scale=x_scale[:, g, t0 + a:t0 + a + width],
-                        start=(g == 0),
-                        stop=(g == PASSES - 1),
-                    )
-                nc.scalar.activation(out=y[:, a:a + width], in_=acc[:], func=GELU)
-                a = a + width
-            nc.vector.tensor_tensor(
-                window[:].indirect(offsets[:, t0 // 16:(t0 + n) // 16]), y[:], gates[i][:], MULT
+        def multiply(acc, t, width, g):
+            i = [k for k, (a, b) in enumerate(WORD_LOADS) if a <= t < b][0]
+            c = t - WORD_LOADS[i][0]
+            nc.tensor.matmul_mx(
+                out=acc[:],
+                lhsT=w_code[g][:].bitcast(FP8X4),
+                lhsT_scale=w_scale[g][:],
+                rhs=x_code[i][:, g, 2 * c:2 * (c + width)].bitcast(FP4X4),
+                rhs_scale=x_scale[:, g, t:t + width],
+                start=(g == 0),
+                stop=(g == PASSES - 1),
             )
-            t0 = t0 + n
+
+        for s, (a, b) in enumerate(pieces):
+            y = keep.tile([P, b - a], F32, name="y%d" % s)
+            starts = [a + sum(GROUPS[s][:j]) for j in range(len(GROUPS[s]))]
+            accs = [psum.tile([P, width], F32, name="acc%d" % t) for t, width in zip(starts, GROUPS[s])]
+            if s == 0:
+                for acc, t, width in zip(accs, starts, GROUPS[s]):
+                    multiply(acc, t, width, 0)
+            for acc, t, width in zip(accs, starts, GROUPS[s]):
+                if s > 0:
+                    multiply(acc, t, width, 0)
+                multiply(acc, t, width, 1)
+                nc.scalar.activation(out=y[:, t - a:t - a + width], in_=acc[:], func=GELU)
+            nc.vector.tensor_tensor(window[:].indirect(offsets[:, a // 16:b // 16]), y[:], gates[s][:], MULT)
 
         nc.sync.dma_start(out=out, in_=window[:])

@@ -66,10 +66,10 @@ def tile_picked_wroute2_lingelu_l_kernel(tc, x_words, x_scales, gate, w1, dst, o
             nc.sync.dma_start(offsets[:], dst)
 
         load_scales(nc.scalar, 0)
+        load_scales(nc.scalar, 1)
         load_weights(0)
         load_weights(1)
         load_codes(0)
-        load_scales(nc.sync, 1)
         load_scales(nc.sync, 2)
         load_scales(nc.sync, 3)
         load_codes(1)

@@ -34,6 +34,8 @@ def tile_picked_wroute2_lingelu_l_kernel(tc, x_words, x_scales, gate, w1, dst, o
 
         offsets = keep.tile([P, T // 16], U16, name="offsets")
         window = keep.tile([P, U], F32, name="window")
+        zero = keep.tile([P, 1], F32, name="zero")
+        nc.vector.memset(zero[:], 0.0)
         nc.vector.memset(window[:], 0.0)
 
         pieces = ((0, FIRST), (FIRST, T))
@@ -69,13 +71,16 @@ def tile_picked_wroute2_lingelu_l_kernel(tc, x_words, x_scales, gate, w1, dst, o
         load_scales(nc.scalar, 1)
         load_weights(0)
         load_weights(1)
-        load_codes(0)
         load_scales(nc.sync, 2)
         load_scales(nc.sync, 3)
+        load_codes(0)
         load_codes(1)
         load_gate(nc.sync, 0)
         load_list()
         load_gate(nc.sync, 1)
+
+        warm = keep.tile([P, 1], F32, name="warm")
+        nc.scalar.activation(out=warm[:], in_=zero[:], func=GELU)
 
         w_code = []
         w_scale = []
@@ -84,11 +89,13 @@ def tile_picked_wroute2_lingelu_l_kernel(tc, x_words, x_scales, gate, w1, dst, o
             codes = keep.tile([P, N], U32, name="w_code%d" % g, align_bytes=64)
             scales = keep.tile([P, N], U8, name="w_scale%d" % g, align_bytes=64)
             halves = [slice(0, N // 2), slice(N // 2, N)]
-            for cols in halves:
-                nc.vector.tensor_copy(
-                    out=grouped[:, cols, :].rearrange("p (c i) t -> p c t i", i=4),
-                    in_=w_raw[g][:, :, cols].rearrange("p t (c i) -> p c t i", i=4),
-                )
+            split = N // 2
+            for copy, cols in ((nc.vector.tensor_copy, slice(0, N // 2)), (nc.vector.tensor_copy, slice(N // 2, split)), (nc.scalar.copy, slice(split, N))):
+                if cols.stop > cols.start:
+                    copy(
+                        out=grouped[:, cols, :].rearrange("p (c i) t -> p c t i", i=4),
+                        in_=w_raw[g][:, :, cols].rearrange("p t (c i) -> p c t i", i=4),
+                    )
             for cols in halves:
                 nc.vector.quantize_mx(
                     out=codes[:, cols].bitcast(FP8X4), scales=scales[:, cols], in_=grouped[:, cols, :].rearrange("p m t -> p (m t)")

@@ -22,7 +22,7 @@ K_PASS = P * PACK
 PASSES = K // K_PASS
 GROUP = 128
 FIRST = 256
-WORD_LOADS = ((0, 256), (256, 1024))
+WORD_LOADS = ((0, 384), (384, 1024))
 GROUPS = ((128, 128), (128,) * 6)
 
 
@@ -34,8 +34,6 @@ def tile_picked_wroute2_lingelu_l_kernel(tc, x_words, x_scales, gate, w1, dst, o
 
         offsets = keep.tile([P, T // 16], U16, name="offsets")
         window = keep.tile([P, U], F32, name="window")
-        zero = keep.tile([P, 1], F32, name="zero")
-        nc.vector.memset(zero[:], 0.0)
         nc.vector.memset(window[:], 0.0)
 
         pieces = ((0, FIRST), (FIRST, T))
@@ -79,9 +77,6 @@ def tile_picked_wroute2_lingelu_l_kernel(tc, x_words, x_scales, gate, w1, dst, o
         load_list()
         load_gate(nc.sync, 1)
 
-        warm = keep.tile([P, 1], F32, name="warm")
-        nc.scalar.activation(out=warm[:], in_=zero[:], func=GELU)
-
         w_code = []
         w_scale = []
         for g in range(PASSES):
@@ -89,13 +84,11 @@ def tile_picked_wroute2_lingelu_l_kernel(tc, x_words, x_scales, gate, w1, dst, o
             codes = keep.tile([P, N], U32, name="w_code%d" % g, align_bytes=64)
             scales = keep.tile([P, N], U8, name="w_scale%d" % g, align_bytes=64)
             halves = [slice(0, N // 2), slice(N // 2, N)]
-            split = N // 2
-            for copy, cols in ((nc.vector.tensor_copy, slice(0, N // 2)), (nc.vector.tensor_copy, slice(N // 2, split)), (nc.scalar.copy, slice(split, N))):
-                if cols.stop > cols.start:
-                    copy(
-                        out=grouped[:, cols, :].rearrange("p (c i) t -> p c t i", i=4),
-                        in_=w_raw[g][:, :, cols].rearrange("p t (c i) -> p c t i", i=4),
-                    )
+            for cols in halves:
+                nc.vector.tensor_copy(
+                    out=grouped[:, cols, :].rearrange("p (c i) t -> p c t i", i=4),
+                    in_=w_raw[g][:, :, cols].rearrange("p t (c i) -> p c t i", i=4),
+                )
             for cols in halves:
                 nc.vector.quantize_mx(
                     out=codes[:, cols].bitcast(FP8X4), scales=scales[:, cols], in_=grouped[:, cols, :].rearrange("p m t -> p (m t)")

@@ -20,9 +20,9 @@ P = 128
 PACK = 4
 K_PASS = P * PACK
 PASSES = K // K_PASS
-GROUP = 128
 FIRST = 256
 WORD_LOADS = ((0, 384), (384, 1024))
+SCALE_LOADS = ((0, 640), (640, 1024))
 GROUPS = ((128, 128), (128,) * 6)
 
 
@@ -39,23 +39,24 @@ def tile_picked_wroute2_lingelu_l_kernel(tc, x_words, x_scales, gate, w1, dst, o
         pieces = ((0, FIRST), (FIRST, T))
         w_raw = [keep.tile([P, PACK, N], F32, name="w_raw%d" % g) for g in range(PASSES)]
         x_code = [keep.tile([P, PASSES, 2 * (b - a)], U8, name="x_code%d" % a, align_bytes=64) for a, b in WORD_LOADS]
-        x_scale = keep.tile([P, PASSES, T], U8, name="x_scale", align_bytes=64)
+        x_scale = [keep.tile([P, PASSES, b - a], U8, name="x_scale%d" % a, align_bytes=64) for a, b in SCALE_LOADS]
         gates = [keep.tile([P, b - a], F32, name="gate%d" % a) for a, b in pieces]
 
         def load_weights(g):
             nc.sync.dma_start(out=w_raw[g][:], in_=w1[g * K_PASS:(g + 1) * K_PASS, :].rearrange("(p j) m -> p j m", j=PACK))
 
-        def load_codes(i):
+        def load_codes(engine, i):
             a, b = WORD_LOADS[i]
-            nc.sync.dma_start(
+            engine.dma_start(
                 out=x_code[i][:].bitcast(I32),
                 in_=x_words[:, :, 2 * a:2 * b].rearrange("z p b -> p z b").bitcast(I32),
             )
 
-        def load_scales(engine, r):
+        def load_scales(engine, i, r):
+            a, b = SCALE_LOADS[i]
             engine.dma_start(
-                out=x_scale[r:P:32, :, :].bitcast(I32),
-                in_=x_scales[:, r:16:4, :].rearrange("z q c -> q z c").bitcast(I32),
+                out=x_scale[i][r:P:32, :, :].bitcast(I32),
+                in_=x_scales[:, r:16:4, a:b].rearrange("z q c -> q z c").bitcast(I32),
             )
 
         def load_gate(engine, i):
@@ -65,16 +66,18 @@ def tile_picked_wroute2_lingelu_l_kernel(tc, x_words, x_scales, gate, w1, dst, o
         def load_list():
             nc.sync.dma_start(offsets[:], dst)
 
-        load_scales(nc.scalar, 0)
-        load_scales(nc.scalar, 1)
+        load_scales(nc.scalar, 0, 0)
+        load_scales(nc.scalar, 0, 1)
         load_weights(0)
         load_weights(1)
-        load_scales(nc.sync, 2)
-        load_scales(nc.sync, 3)
-        load_codes(0)
-        load_codes(1)
+        load_scales(nc.sync, 0, 2)
+        load_scales(nc.sync, 0, 3)
+        load_codes(nc.sync, 0)
+        load_codes(nc.sync, 1)
         load_gate(nc.sync, 0)
         load_list()
+        for r in range(4):
+            load_scales(nc.sync, 1, r)
         load_gate(nc.sync, 1)
 
         w_code = []
@@ -99,12 +102,14 @@ def tile_picked_wroute2_lingelu_l_kernel(tc, x_words, x_scales, gate, w1, dst, o
         def multiply(acc, t, width, g):
             i = [k for k, (a, b) in enumerate(WORD_LOADS) if a <= t < b][0]
             c = t - WORD_LOADS[i][0]
+            j = [k for k, (a, b) in enumerate(SCALE_LOADS) if a <= t < b][0]
+            d = t - SCALE_LOADS[j][0]
             nc.tensor.matmul_mx(
                 out=acc[:],
                 lhsT=w_code[g][:].bitcast(FP8X4),
                 lhsT_scale=w_scale[g][:],
                 rhs=x_code[i][:, g, 2 * c:2 * (c + width)].bitcast(FP4X4),
-                rhs_scale=x_scale[:, g, t:t + width],
+                rhs_scale=x_scale[j][:, g, d:d + width],
                 start=(g == 0),
                 stop=(g == PASSES - 1),
             )

@@ -21,8 +21,8 @@ PACK = 4
 K_PASS = P * PACK
 PASSES = K // K_PASS
 FIRST = 256
-WORD_LOADS = ((0, 384), (384, 1024))
-SCALE_LOADS = ((0, 640), (640, 1024))
+WORD_LOADS = ((0, 256), (256, 1024))
+ROW_SPLIT = (384, 512, 640, 640)
 GROUPS = ((128, 128), (128,) * 6)
 
 
@@ -39,7 +39,7 @@ def tile_picked_wroute2_lingelu_l_kernel(tc, x_words, x_scales, gate, w1, dst, o
         pieces = ((0, FIRST), (FIRST, T))
         w_raw = [keep.tile([P, PACK, N], F32, name="w_raw%d" % g) for g in range(PASSES)]
         x_code = [keep.tile([P, PASSES, 2 * (b - a)], U8, name="x_code%d" % a, align_bytes=64) for a, b in WORD_LOADS]
-        x_scale = [keep.tile([P, PASSES, b - a], U8, name="x_scale%d" % a, align_bytes=64) for a, b in SCALE_LOADS]
+        x_scale = keep.tile([P, PASSES, T], U8, name="x_scale", align_bytes=64)
         gates = [keep.tile([P, b - a], F32, name="gate%d" % a) for a, b in pieces]
 
         def load_weights(g):
@@ -53,9 +53,9 @@ def tile_picked_wroute2_lingelu_l_kernel(tc, x_words, x_scales, gate, w1, dst, o
             )
 
         def load_scales(engine, i, r):
-            a, b = SCALE_LOADS[i]
+            a, b = ((0, ROW_SPLIT[r]), (ROW_SPLIT[r], T))[i]
             engine.dma_start(
-                out=x_scale[i][r:P:32, :, :].bitcast(I32),
+                out=x_scale[r:P:32, :, a:b].bitcast(I32),
                 in_=x_scales[:, r:16:4, a:b].rearrange("z q c -> q z c").bitcast(I32),
             )
 
@@ -102,14 +102,12 @@ def tile_picked_wroute2_lingelu_l_kernel(tc, x_words, x_scales, gate, w1, dst, o
         def multiply(acc, t, width, g):
             i = [k for k, (a, b) in enumerate(WORD_LOADS) if a <= t < b][0]
             c = t - WORD_LOADS[i][0]
-            j = [k for k, (a, b) in enumerate(SCALE_LOADS) if a <= t < b][0]
-            d = t - SCALE_LOADS[j][0]
             nc.tensor.matmul_mx(
                 out=acc[:],
                 lhsT=w_code[g][:].bitcast(FP8X4),
                 lhsT_scale=w_scale[g][:],
                 rhs=x_code[i][:, g, 2 * c:2 * (c + width)].bitcast(FP4X4),
-                rhs_scale=x_scale[j][:, g, d:d + width],
+                rhs_scale=x_scale[:, g, t:t + width],
                 start=(g == 0),
                 stop=(g == PASSES - 1),
             )

@@ -14,7 +14,9 @@ U8 = mybir.dt.uint8
 FP8X4 = mybir.dt.float8_e4m3fn_x4
 FP4X4 = mybir.dt.float4_e2m1fn_x4
 GELU = mybir.ActivationFunctionType.Gelu_apprx_tanh
+COPY = mybir.ActivationFunctionType.Copy
 MULT = mybir.AluOpType.mult
+ADD = mybir.AluOpType.add
 
 P = 128
 PACK = 4
@@ -23,7 +25,9 @@ PASSES = K // K_PASS
 FIRST = 256
 WORD_LOADS = ((0, 256), (256, 1024))
 ROW_SPLIT = (384, 512, 640, 640)
-GROUPS = ((128, 128), (128,) * 6)
+GROUP = 128
+SHARE = 384
+STORES = (512, 512, 512, 512)
 
 
 def tile_picked_wroute2_lingelu_l_kernel(tc, x_words, x_scales, gate, w1, dst, out):
@@ -35,6 +39,8 @@ def tile_picked_wroute2_lingelu_l_kernel(tc, x_words, x_scales, gate, w1, dst, o
         offsets = keep.tile([P, T // 16], U16, name="offsets")
         window = keep.tile([P, U], F32, name="window")
         nc.vector.memset(window[:], 0.0)
+        side = keep.tile([P, U], F32, name="side")
+        nc.gpsimd.memset(side[:, 0:U // 4], 0.0)
 
         pieces = ((0, FIRST), (FIRST, T))
         w_raw = [keep.tile([P, PACK, N], F32, name="w_raw%d" % g) for g in range(PASSES)]
@@ -80,6 +86,12 @@ def tile_picked_wroute2_lingelu_l_kernel(tc, x_words, x_scales, gate, w1, dst, o
             load_scales(nc.sync, 1, r)
         load_gate(nc.sync, 1)
 
+        nc.scalar.activation(
+            out=side[:, U // 4:].rearrange("p (r c) -> p r c", r=3),
+            in_=side[:, 0:U // 4].unsqueeze(1).to_broadcast([P, 3, U // 4]),
+            func=GELU,
+        )
+
         w_code = []
         w_scale = []
         for g in range(PASSES):
@@ -112,18 +124,37 @@ def tile_picked_wroute2_lingelu_l_kernel(tc, x_words, x_scales, gate, w1, dst, o
                 stop=(g == PASSES - 1),
             )
 
-        for s, (a, b) in enumerate(pieces):
-            y = keep.tile([P, b - a], F32, name="y%d" % s)
-            starts = [a + sum(GROUPS[s][:j]) for j in range(len(GROUPS[s]))]
-            accs = [psum.tile([P, width], F32, name="acc%d" % t) for t, width in zip(starts, GROUPS[s])]
-            if s == 0:
-                for acc, t, width in zip(accs, starts, GROUPS[s]):
-                    multiply(acc, t, width, 0)
-            for acc, t, width in zip(accs, starts, GROUPS[s]):
-                if s > 0:
-                    multiply(acc, t, width, 0)
-                multiply(acc, t, width, 1)
-                nc.scalar.activation(out=y[:, t - a:t - a + width], in_=acc[:], func=GELU)
-            nc.vector.tensor_tensor(window[:].indirect(offsets[:, a // 16:b // 16]), y[:], gates[s][:], MULT)
+        accs = {t: psum.tile([P, GROUP], F32, name="acc%d" % t) for t in range(0, T, GROUP)}
+        mid = FIRST + SHARE
+        y_first = keep.tile([P, FIRST], F32, name="y_first")
+        y_side = keep.tile([P, SHARE], F32, name="y_side")
+        y_last = keep.tile([P, T - mid], F32, name="y_last")
+        gated = keep.tile([P, SHARE], F32, name="gated")
 
-        nc.sync.dma_start(out=out, in_=window[:])
+        def activate(t):
+            y, a = (y_first, 0) if t < FIRST else (y_side, FIRST) if t < mid else (y_last, mid)
+            nc.scalar.activation(out=y[:, t - a:t - a + GROUP], in_=accs[t][:], func=GELU)
+
+        for t in range(0, FIRST, GROUP):
+            multiply(accs[t], t, GROUP, 0)
+        for t in range(0, FIRST, GROUP):
+            multiply(accs[t], t, GROUP, 1)
+            activate(t)
+        nc.vector.tensor_tensor(window[:].indirect(offsets[:, 0:FIRST // 16]), y_first[:], gates[0][:], MULT)
+
+        side_groups = list(range(FIRST, mid, GROUP))
+        last_groups = list(range(mid, T, GROUP))
+        for t in side_groups[:-1] + last_groups[:-1] + side_groups[-1:] + last_groups[-1:]:
+            multiply(accs[t], t, GROUP, 0)
+            multiply(accs[t], t, GROUP, 1)
+            activate(t)
+        nc.vector.tensor_tensor(gated[:], y_side[:], gates[1][:, 0:SHARE], MULT)
+        nc.vector.tensor_tensor(window[:].indirect(offsets[:, mid // 16:T // 16]), y_last[:], gates[1][:, SHARE:], MULT)
+        nc.scalar.activation(out=side[:].indirect(offsets[:, FIRST // 16:mid // 16]), in_=gated[:], func=COPY)
+
+        a = 0
+        for width in STORES:
+            total = keep.tile([P, width], F32, name="total%d" % a)
+            nc.vector.tensor_tensor(total[:], window[:, a:a + width], side[:, a:a + width], ADD)
+            nc.sync.dma_start(out=out[:, a:a + width], in_=total[:])
+            a += width

@@ -22,11 +22,11 @@ P = 128
 PACK = 4
 K_PASS = P * PACK
 PASSES = K // K_PASS
-FIRST = 256
-WORD_LOADS = ((0, 256), (256, 1024))
-ROW_SPLIT = (384, 512, 640, 640)
-GROUP = 128
-SHARE = 384
+PIECE = 256
+WORD_LOADS = ((0, 256), (256, 512), (512, 1024))
+GATE_LOADS = ((0, 256), (256, 512), (512, 1024))
+ROW_SPLIT = (512, 512, 512, 512)
+GROUPS = ((128, 128), (128, 128), (128, 128), (256,))
 STORES = (512, 512, 512, 512)
 
 
@@ -38,15 +38,14 @@ def tile_picked_wroute2_lingelu_l_kernel(tc, x_words, x_scales, gate, w1, dst, o
 
         offsets = keep.tile([P, T // 16], U16, name="offsets")
         window = keep.tile([P, U], F32, name="window")
-        nc.vector.memset(window[:], 0.0)
         side = keep.tile([P, U], F32, name="side")
+        nc.vector.memset(window[:], 0.0)
         nc.gpsimd.memset(side[:, 0:U // 4], 0.0)
 
-        pieces = ((0, FIRST), (FIRST, T))
         w_raw = [keep.tile([P, PACK, N], F32, name="w_raw%d" % g) for g in range(PASSES)]
         x_code = [keep.tile([P, PASSES, 2 * (b - a)], U8, name="x_code%d" % a, align_bytes=64) for a, b in WORD_LOADS]
         x_scale = keep.tile([P, PASSES, T], U8, name="x_scale", align_bytes=64)
-        gates = [keep.tile([P, b - a], F32, name="gate%d" % a) for a, b in pieces]
+        gates = [keep.tile([P, b - a], F32, name="gate%d" % a) for a, b in GATE_LOADS]
 
         def load_weights(g):
             nc.sync.dma_start(out=w_raw[g][:], in_=w1[g * K_PASS:(g + 1) * K_PASS, :].rearrange("(p j) m -> p j m", j=PACK))
@@ -66,7 +65,7 @@ def tile_picked_wroute2_lingelu_l_kernel(tc, x_words, x_scales, gate, w1, dst, o
             )
 
         def load_gate(engine, i):
-            a, b = pieces[i]
+            a, b = GATE_LOADS[i]
             engine.dma_start(out=gates[i][:], in_=gate[:, a:b])
 
         def load_list():
@@ -82,9 +81,13 @@ def tile_picked_wroute2_lingelu_l_kernel(tc, x_words, x_scales, gate, w1, dst, o
         load_codes(nc.sync, 1)
         load_gate(nc.sync, 0)
         load_list()
-        for r in range(4):
-            load_scales(nc.sync, 1, r)
         load_gate(nc.sync, 1)
+        load_codes(nc.sync, 2)
+        load_scales(nc.sync, 1, 0)
+        load_scales(nc.sync, 1, 1)
+        load_scales(nc.sync, 1, 2)
+        load_scales(nc.sync, 1, 3)
+        load_gate(nc.sync, 2)
 
         nc.scalar.activation(
             out=side[:, U // 4:].rearrange("p (r c) -> p r c", r=3),
@@ -124,33 +127,32 @@ def tile_picked_wroute2_lingelu_l_kernel(tc, x_words, x_scales, gate, w1, dst, o
                 stop=(g == PASSES - 1),
             )
 
-        accs = {t: psum.tile([P, GROUP], F32, name="acc%d" % t) for t in range(0, T, GROUP)}
-        mid = FIRST + SHARE
-        y_first = keep.tile([P, FIRST], F32, name="y_first")
-        y_side = keep.tile([P, SHARE], F32, name="y_side")
-        y_last = keep.tile([P, T - mid], F32, name="y_last")
-        gated = keep.tile([P, SHARE], F32, name="gated")
+        def gate_of(a, b):
+            i = [k for k, (lo, hi) in enumerate(GATE_LOADS) if lo <= a < hi][0]
+            return gates[i][:, a - GATE_LOADS[i][0]:b - GATE_LOADS[i][0]]
 
-        def activate(t):
-            y, a = (y_first, 0) if t < FIRST else (y_side, FIRST) if t < mid else (y_last, mid)
-            nc.scalar.activation(out=y[:, t - a:t - a + GROUP], in_=accs[t][:], func=GELU)
-
-        for t in range(0, FIRST, GROUP):
-            multiply(accs[t], t, GROUP, 0)
-        for t in range(0, FIRST, GROUP):
-            multiply(accs[t], t, GROUP, 1)
-            activate(t)
-        nc.vector.tensor_tensor(window[:].indirect(offsets[:, 0:FIRST // 16]), y_first[:], gates[0][:], MULT)
-
-        side_groups = list(range(FIRST, mid, GROUP))
-        last_groups = list(range(mid, T, GROUP))
-        for t in side_groups[:-1] + last_groups[:-1] + side_groups[-1:] + last_groups[-1:]:
-            multiply(accs[t], t, GROUP, 0)
-            multiply(accs[t], t, GROUP, 1)
-            activate(t)
-        nc.vector.tensor_tensor(gated[:], y_side[:], gates[1][:, 0:SHARE], MULT)
-        nc.vector.tensor_tensor(window[:].indirect(offsets[:, mid // 16:T // 16]), y_last[:], gates[1][:, SHARE:], MULT)
-        nc.scalar.activation(out=side[:].indirect(offsets[:, FIRST // 16:mid // 16]), in_=gated[:], func=COPY)
+        for s in range(T // PIECE):
+            a, b = s * PIECE, (s + 1) * PIECE
+            y = keep.tile([P, PIECE], F32, name="y%d" % s)
+            gated = keep.tile([P, PIECE], F32, name="gated%d" % s) if s % 2 == 0 else None
+            starts = [a + sum(GROUPS[s][:j]) for j in range(len(GROUPS[s]))]
+            accs = [psum.tile([P, width], F32, name="acc%d" % t) for t, width in zip(starts, GROUPS[s])]
+            if s == 0:
+                for acc, t, width in zip(accs, starts, GROUPS[s]):
+                    multiply(acc, t, width, 0)
+            for acc, t, width in zip(accs, starts, GROUPS[s]):
+                if s > 0:
+                    multiply(acc, t, width, 0)
+                multiply(acc, t, width, 1)
+                cols = slice(t - a, t - a + width)
+                nc.scalar.activation(out=y[:, cols], in_=acc[:], func=GELU)
+                if s % 2 == 0:
+                    nc.vector.tensor_tensor(gated[:, cols], y[:, cols], gate_of(t, t + width), MULT)
+            places = offsets[:, a // 16:b // 16]
+            if s % 2 == 0:
+                nc.scalar.activation(out=side[:].indirect(places), in_=gated[:], func=COPY)
+            else:
+                nc.vector.tensor_tensor(window[:].indirect(places), y[:], gate_of(a, b), MULT)
 
         a = 0
         for width in STORES:

@@ -27,7 +27,9 @@ WORD_LOADS = ((0, 256), (256, 512), (512, 1024))
 GATE_LOADS = ((0, 256), (256, 512), (512, 1024))
 ROW_SPLIT = (512, 512, 512, 512)
 GROUPS = ((128, 128), (128, 128), (128, 128), (256,))
-STORES = (512, 512, 512, 512)
+SEED = 256
+CLEAR = 1024
+STORES = (256, 256, 512, 512, 512)
 
 
 def tile_picked_wroute2_lingelu_l_kernel(tc, x_words, x_scales, gate, w1, dst, out):
@@ -39,8 +41,15 @@ def tile_picked_wroute2_lingelu_l_kernel(tc, x_words, x_scales, gate, w1, dst, o
         offsets = keep.tile([P, T // 16], U16, name="offsets")
         window = keep.tile([P, U], F32, name="window")
         side = keep.tile([P, U], F32, name="side")
-        nc.vector.memset(window[:], 0.0)
-        nc.gpsimd.memset(side[:, 0:U // 4], 0.0)
+        seed = keep.tile([P, SEED], F32, name="seed")
+        nc.vector.memset(seed[:], 0.0)
+        zeros = seed[:].unsqueeze(1)
+
+        def runs(ap):
+            return ap.rearrange("p (r c) -> p r c", c=SEED)
+
+        nc.vector.tensor_copy(out=runs(window[:]), in_=zeros.to_broadcast([P, U // SEED, SEED]))
+        nc.vector.tensor_copy(out=runs(side[:, 0:CLEAR]), in_=zeros.to_broadcast([P, CLEAR // SEED, SEED]))
 
         w_raw = [keep.tile([P, PACK, N], F32, name="w_raw%d" % g) for g in range(PASSES)]
         x_code = [keep.tile([P, PASSES, 2 * (b - a)], U8, name="x_code%d" % a, align_bytes=64) for a, b in WORD_LOADS]
@@ -89,11 +98,7 @@ def tile_picked_wroute2_lingelu_l_kernel(tc, x_words, x_scales, gate, w1, dst, o
         load_scales(nc.sync, 1, 3)
         load_gate(nc.sync, 2)
 
-        nc.scalar.activation(
-            out=side[:, U // 4:].rearrange("p (r c) -> p r c", r=3),
-            in_=side[:, 0:U // 4].unsqueeze(1).to_broadcast([P, 3, U // 4]),
-            func=GELU,
-        )
+        nc.scalar.activation(out=runs(side[:, CLEAR:]), in_=zeros.to_broadcast([P, (U - CLEAR) // SEED, SEED]), func=GELU)
 
         w_code = []
         w_scale = []

@@ -23,12 +23,11 @@ PACK = 4
 K_PASS = P * PACK
 PASSES = K // K_PASS
 PIECE = 256
-WORD_LOADS = ((0, 256), (256, 512), (512, 1024))
+GROUP = 128
+EARLY = 512
 GATE_LOADS = ((0, 256), (256, 512), (512, 1024))
-ROW_SPLIT = (512, 512, 512, 512)
-GROUPS = ((128, 128), (128, 128), (128, 128), (256,))
 SEED = 256
-CLEAR = 1024
+CLEAR = 512
 STORES = (256, 256, 512, 512, 512)
 
 
@@ -52,51 +51,45 @@ def tile_picked_wroute2_lingelu_l_kernel(tc, x_words, x_scales, gate, w1, dst, o
         nc.vector.tensor_copy(out=runs(side[:, 0:CLEAR]), in_=zeros.to_broadcast([P, CLEAR // SEED, SEED]))
 
         w_raw = [keep.tile([P, PACK, N], F32, name="w_raw%d" % g) for g in range(PASSES)]
-        x_code = [keep.tile([P, PASSES, 2 * (b - a)], U8, name="x_code%d" % a, align_bytes=64) for a, b in WORD_LOADS]
+        early = [keep.tile([P, 2 * EARLY], U8, name="early%d" % g, align_bytes=64) for g in range(PASSES)]
+        late = keep.tile([P, PASSES, 2 * (T - EARLY)], U8, name="late", align_bytes=64)
         x_scale = keep.tile([P, PASSES, T], U8, name="x_scale", align_bytes=64)
         gates = [keep.tile([P, b - a], F32, name="gate%d" % a) for a, b in GATE_LOADS]
 
         def load_weights(g):
             nc.sync.dma_start(out=w_raw[g][:], in_=w1[g * K_PASS:(g + 1) * K_PASS, :].rearrange("(p j) m -> p j m", j=PACK))
 
-        def load_codes(engine, i):
-            a, b = WORD_LOADS[i]
-            engine.dma_start(
-                out=x_code[i][:].bitcast(I32),
-                in_=x_words[:, :, 2 * a:2 * b].rearrange("z p b -> p z b").bitcast(I32),
-            )
+        def load_early(g):
+            nc.sync.dma_start(out=early[g][:].bitcast(I32), in_=x_words[g, :, 0:2 * EARLY].bitcast(I32))
 
-        def load_scales(engine, i, r):
-            a, b = ((0, ROW_SPLIT[r]), (ROW_SPLIT[r], T))[i]
+        def load_late():
+            nc.sync.dma_start(out=late[:].bitcast(I32), in_=x_words[:, :, 2 * EARLY:2 * T].rearrange("z p b -> p z b").bitcast(I32))
+
+        def load_scales(engine, r, a, b):
             engine.dma_start(
                 out=x_scale[r:P:32, :, a:b].bitcast(I32),
                 in_=x_scales[:, r:16:4, a:b].rearrange("z q c -> q z c").bitcast(I32),
             )
 
-        def load_gate(engine, i):
+        def load_gate(i):
             a, b = GATE_LOADS[i]
-            engine.dma_start(out=gates[i][:], in_=gate[:, a:b])
+            nc.sync.dma_start(out=gates[i][:], in_=gate[:, a:b])
 
-        def load_list():
-            nc.sync.dma_start(offsets[:], dst)
-
-        load_scales(nc.scalar, 0, 0)
-        load_scales(nc.scalar, 0, 1)
+        load_scales(nc.scalar, 0, 0, EARLY)
+        load_scales(nc.scalar, 1, 0, EARLY)
         load_weights(0)
         load_weights(1)
-        load_scales(nc.sync, 0, 2)
-        load_scales(nc.sync, 0, 3)
-        load_codes(nc.sync, 0)
-        load_codes(nc.sync, 1)
-        load_gate(nc.sync, 0)
-        load_list()
-        load_gate(nc.sync, 1)
-        load_codes(nc.sync, 2)
-        load_scales(nc.sync, 1, 0)
-        load_scales(nc.sync, 1, 1)
-        load_scales(nc.sync, 1, 2)
-        load_scales(nc.sync, 1, 3)
-        load_gate(nc.sync, 2)
+        load_scales(nc.sync, 2, 0, EARLY)
+        load_scales(nc.sync, 3, 0, EARLY)
+        load_early(0)
+        load_early(1)
+        load_gate(0)
+        nc.sync.dma_start(offsets[:], dst)
+        load_gate(1)
+        load_late()
+        for r in range(4):
+            load_scales(nc.sync, r, EARLY, T)
+        load_gate(2)
 
         nc.scalar.activation(out=runs(side[:, CLEAR:]), in_=zeros.to_broadcast([P, (U - CLEAR) // SEED, SEED]), func=GELU)
 
@@ -119,14 +112,21 @@ def tile_picked_wroute2_lingelu_l_kernel(tc, x_words, x_scales, gate, w1, dst, o
             w_code.append(codes)
             w_scale.append(scales)
 
-        def multiply(acc, t, width, g):
-            i = [k for k, (a, b) in enumerate(WORD_LOADS) if a <= t < b][0]
-            c = t - WORD_LOADS[i][0]
+        groups = ((0, 128), (128, 128), (256, 128), (384, 128), (512, 128), (640, 128), (768, 256))
+        accs = {t: psum.tile([P, width], F32, name="acc%d" % t) for t, width in groups}
+        widths = dict(groups)
+
+        def multiply(t, g):
+            width = widths[t]
+            if t < EARLY:
+                words = early[g][:, 2 * t:2 * (t + width)]
+            else:
+                words = late[:, g, 2 * (t - EARLY):2 * (t - EARLY + width)]
             nc.tensor.matmul_mx(
-                out=acc[:],
+                out=accs[t][:],
                 lhsT=w_code[g][:].bitcast(FP8X4),
                 lhsT_scale=w_scale[g][:],
-                rhs=x_code[i][:, g, 2 * c:2 * (c + width)].bitcast(FP4X4),
+                rhs=words.bitcast(FP4X4),
                 rhs_scale=x_scale[:, g, t:t + width],
                 start=(g == 0),
                 stop=(g == PASSES - 1),
@@ -136,28 +136,40 @@ def tile_picked_wroute2_lingelu_l_kernel(tc, x_words, x_scales, gate, w1, dst, o
             i = [k for k, (lo, hi) in enumerate(GATE_LOADS) if lo <= a < hi][0]
             return gates[i][:, a - GATE_LOADS[i][0]:b - GATE_LOADS[i][0]]
 
-        for s in range(T // PIECE):
+        ys = [keep.tile([P, PIECE], F32, name="y%d" % s) for s in range(T // PIECE)]
+        gated = {s: keep.tile([P, PIECE], F32, name="gated%d" % s) for s in (0, 2)}
+
+        def finish(t):
+            width = widths[t]
+            s, c = divmod(t, PIECE)
+            nc.scalar.activation(out=ys[s][:, c:c + width], in_=accs[t][:], func=GELU)
+            if s in gated:
+                nc.vector.tensor_tensor(gated[s][:, c:c + width], ys[s][:, c:c + width], gate_of(t, t + width), MULT)
+
+        def scatter(s):
             a, b = s * PIECE, (s + 1) * PIECE
-            y = keep.tile([P, PIECE], F32, name="y%d" % s)
-            gated = keep.tile([P, PIECE], F32, name="gated%d" % s) if s % 2 == 0 else None
-            starts = [a + sum(GROUPS[s][:j]) for j in range(len(GROUPS[s]))]
-            accs = [psum.tile([P, width], F32, name="acc%d" % t) for t, width in zip(starts, GROUPS[s])]
-            if s == 0:
-                for acc, t, width in zip(accs, starts, GROUPS[s]):
-                    multiply(acc, t, width, 0)
-            for acc, t, width in zip(accs, starts, GROUPS[s]):
-                if s > 0:
-                    multiply(acc, t, width, 0)
-                multiply(acc, t, width, 1)
-                cols = slice(t - a, t - a + width)
-                nc.scalar.activation(out=y[:, cols], in_=acc[:], func=GELU)
-                if s % 2 == 0:
-                    nc.vector.tensor_tensor(gated[:, cols], y[:, cols], gate_of(t, t + width), MULT)
             places = offsets[:, a // 16:b // 16]
-            if s % 2 == 0:
-                nc.scalar.activation(out=side[:].indirect(places), in_=gated[:], func=COPY)
+            if s in gated:
+                nc.scalar.activation(out=side[:].indirect(places), in_=gated[s][:], func=COPY)
             else:
-                nc.vector.tensor_tensor(window[:].indirect(places), y[:], gate_of(a, b), MULT)
+                nc.vector.tensor_tensor(window[:].indirect(places), ys[s][:], gate_of(a, b), MULT)
+
+        for t in (0, 128, 256):
+            multiply(t, 0)
+        for t in (0, 128, 256, 384):
+            if t == 384:
+                multiply(t, 0)
+            multiply(t, 1)
+            finish(t)
+        scatter(0)
+        scatter(1)
+        for t in (512, 640, 768):
+            multiply(t, 0)
+            multiply(t, 1)
+            finish(t)
+        scatter(2)
+        scatter(3)
+
 
         a = 0
         for width in STORES:

@@ -26,8 +26,9 @@ PIECE = 256
 GROUP = 128
 EARLY = 512
 GATE_LOADS = ((0, 256), (256, 512), (512, 1024))
-SEED = 256
-CLEAR = 512
+SEED = 128
+LATE_CLEAR = 512
+CLEAR = 1280
 STORES = (256, 256, 512, 512, 512)
 
 
@@ -47,7 +48,7 @@ def tile_picked_wroute2_lingelu_l_kernel(tc, x_words, x_scales, gate, w1, dst, o
         def runs(ap):
             return ap.rearrange("p (r c) -> p r c", c=SEED)
 
-        nc.vector.tensor_copy(out=runs(window[:]), in_=zeros.to_broadcast([P, U // SEED, SEED]))
+        nc.vector.tensor_copy(out=runs(window[:, LATE_CLEAR:]), in_=zeros.to_broadcast([P, (U - LATE_CLEAR) // SEED, SEED]))
         nc.vector.tensor_copy(out=runs(side[:, 0:CLEAR]), in_=zeros.to_broadcast([P, CLEAR // SEED, SEED]))
 
         w_raw = [keep.tile([P, PACK, N], F32, name="w_raw%d" % g) for g in range(PASSES)]
@@ -96,7 +97,7 @@ def tile_picked_wroute2_lingelu_l_kernel(tc, x_words, x_scales, gate, w1, dst, o
         w_code = []
         w_scale = []
         for g in range(PASSES):
-            grouped = keep.tile([P, N, PACK], BF16, name="grouped%d" % g, align_bytes=64)
+            grouped = keep.tile([P, N, PACK], BF16, name="grouped%d" % g, tag="pass%d" % g, align_bytes=64)
             codes = keep.tile([P, N], U32, name="w_code%d" % g, align_bytes=64)
             scales = keep.tile([P, N], U8, name="w_scale%d" % g, align_bytes=64)
             halves = [slice(0, N // 2), slice(N // 2, N)]
@@ -111,6 +112,10 @@ def tile_picked_wroute2_lingelu_l_kernel(tc, x_words, x_scales, gate, w1, dst, o
                 )
             w_code.append(codes)
             w_scale.append(scales)
+
+        late_seed = keep.tile([P, SEED], F32, name="late_seed", tag="pass1", align_bytes=64)
+        nc.vector.memset(late_seed[:], 0.0)
+        nc.vector.tensor_copy(out=runs(window[:, 0:LATE_CLEAR]), in_=late_seed[:].unsqueeze(1).to_broadcast([P, LATE_CLEAR // SEED, SEED]))
 
         groups = ((0, 128), (128, 128), (256, 128), (384, 128), (512, 128), (640, 128), (768, 256))
         accs = {t: psum.tile([P, width], F32, name="acc%d" % t) for t, width in groups}

@@ -24,7 +24,7 @@ K_PASS = P * PACK
 PASSES = K // K_PASS
 PIECE = 256
 GROUP = 128
-EARLY = 512
+EARLY = 768
 GATE_LOADS = ((0, 256), (256, 512), (512, 1024))
 SEED = 128
 LATE_CLEAR = 512
@@ -79,10 +79,10 @@ def tile_picked_wroute2_lingelu_l_kernel(tc, x_words, x_scales, gate, w1, dst, o
         load_scales(nc.scalar, 0, 0, EARLY)
         load_scales(nc.scalar, 1, 0, EARLY)
         load_weights(0)
-        load_weights(1)
         load_scales(nc.sync, 2, 0, EARLY)
         load_scales(nc.sync, 3, 0, EARLY)
         load_early(0)
+        load_weights(1)
         load_early(1)
         load_gate(0)
         nc.sync.dma_start(offsets[:], dst)
@@ -117,7 +117,7 @@ def tile_picked_wroute2_lingelu_l_kernel(tc, x_words, x_scales, gate, w1, dst, o
         nc.vector.memset(late_seed[:], 0.0)
         nc.vector.tensor_copy(out=runs(window[:, 0:LATE_CLEAR]), in_=late_seed[:].unsqueeze(1).to_broadcast([P, LATE_CLEAR // SEED, SEED]))
 
-        groups = ((0, 128), (128, 128), (256, 128), (384, 128), (512, 128), (640, 128), (768, 256))
+        groups = ((0, 128), (128, 128), (256, 256), (512, 256), (768, 256))
         accs = {t: psum.tile([P, width], F32, name="acc%d" % t) for t, width in groups}
         widths = dict(groups)
 
@@ -148,7 +148,7 @@ def tile_picked_wroute2_lingelu_l_kernel(tc, x_words, x_scales, gate, w1, dst, o
             width = widths[t]
             s, c = divmod(t, PIECE)
             nc.scalar.activation(out=ys[s][:, c:c + width], in_=accs[t][:], func=GELU)
-            if s in gated:
+            if s == 0:
                 nc.vector.tensor_tensor(gated[s][:, c:c + width], ys[s][:, c:c + width], gate_of(t, t + width), MULT)
 
         def scatter(s):
@@ -159,22 +159,19 @@ def tile_picked_wroute2_lingelu_l_kernel(tc, x_words, x_scales, gate, w1, dst, o
             else:
                 nc.vector.tensor_tensor(window[:].indirect(places), ys[s][:], gate_of(a, b), MULT)
 
-        for t in (0, 128, 256):
+        for t in (0, 128, 256, 512):
             multiply(t, 0)
-        for t in (0, 128, 256, 384):
-            if t == 384:
-                multiply(t, 0)
+        for t in (0, 128, 256, 512):
             multiply(t, 1)
             finish(t)
         scatter(0)
         scatter(1)
-        for t in (512, 640, 768):
-            multiply(t, 0)
-            multiply(t, 1)
-            finish(t)
+        nc.vector.tensor_tensor(gated[2][:], ys[2][:], gate_of(512, 768), MULT)
+        multiply(EARLY, 0)
+        multiply(EARLY, 1)
+        finish(EARLY)
         scatter(2)
         scatter(3)
-
 
         a = 0
         for width in STORES:

@@ -24,7 +24,8 @@ K_PASS = P * PACK
 PASSES = K // K_PASS
 PIECE = 256
 GROUP = 128
-EARLY = 768
+EARLY = 512
+AHEAD = 768
 GATE_LOADS = ((0, 256), (256, 512), (512, 1024))
 SEED = 128
 LATE_CLEAR = 512
@@ -53,7 +54,8 @@ def tile_picked_wroute2_lingelu_l_kernel(tc, x_words, x_scales, gate, w1, dst, o
 
         w_raw = [keep.tile([P, PACK, N], F32, name="w_raw%d" % g) for g in range(PASSES)]
         early = [keep.tile([P, 2 * EARLY], U8, name="early%d" % g, align_bytes=64) for g in range(PASSES)]
-        late = keep.tile([P, PASSES, 2 * (T - EARLY)], U8, name="late", align_bytes=64)
+        middle = keep.tile([P, PASSES, 2 * (AHEAD - EARLY)], U8, name="middle", align_bytes=64)
+        late = keep.tile([P, PASSES, 2 * (T - AHEAD)], U8, name="late", align_bytes=64)
         x_scale = keep.tile([P, PASSES, T], U8, name="x_scale", align_bytes=64)
         gates = [keep.tile([P, b - a], F32, name="gate%d" % a) for a, b in GATE_LOADS]
 
@@ -63,8 +65,8 @@ def tile_picked_wroute2_lingelu_l_kernel(tc, x_words, x_scales, gate, w1, dst, o
         def load_early(g):
             nc.sync.dma_start(out=early[g][:].bitcast(I32), in_=x_words[g, :, 0:2 * EARLY].bitcast(I32))
 
-        def load_late():
-            nc.sync.dma_start(out=late[:].bitcast(I32), in_=x_words[:, :, 2 * EARLY:2 * T].rearrange("z p b -> p z b").bitcast(I32))
+        def load_both(tile, a, b):
+            nc.sync.dma_start(out=tile[:].bitcast(I32), in_=x_words[:, :, 2 * a:2 * b].rearrange("z p b -> p z b").bitcast(I32))
 
         def load_scales(engine, r, a, b):
             engine.dma_start(
@@ -76,20 +78,21 @@ def tile_picked_wroute2_lingelu_l_kernel(tc, x_words, x_scales, gate, w1, dst, o
             a, b = GATE_LOADS[i]
             nc.sync.dma_start(out=gates[i][:], in_=gate[:, a:b])
 
-        load_scales(nc.scalar, 0, 0, EARLY)
-        load_scales(nc.scalar, 1, 0, EARLY)
+        load_scales(nc.scalar, 0, 0, AHEAD)
+        load_scales(nc.scalar, 1, 0, AHEAD)
         load_weights(0)
-        load_scales(nc.sync, 2, 0, EARLY)
-        load_scales(nc.sync, 3, 0, EARLY)
-        load_early(0)
         load_weights(1)
+        load_scales(nc.sync, 2, 0, AHEAD)
+        load_scales(nc.sync, 3, 0, AHEAD)
+        load_early(0)
         load_early(1)
+        load_both(middle, EARLY, AHEAD)
         load_gate(0)
-        nc.sync.dma_start(offsets[:], dst)
         load_gate(1)
-        load_late()
+        load_both(late, AHEAD, T)
+        nc.sync.dma_start(offsets[:], dst)
         for r in range(4):
-            load_scales(nc.sync, r, EARLY, T)
+            load_scales(nc.sync, r, AHEAD, T)
         load_gate(2)
 
         nc.scalar.activation(out=runs(side[:, CLEAR:]), in_=zeros.to_broadcast([P, (U - CLEAR) // SEED, SEED]), func=GELU)
@@ -117,7 +120,7 @@ def tile_picked_wroute2_lingelu_l_kernel(tc, x_words, x_scales, gate, w1, dst, o
         nc.vector.memset(late_seed[:], 0.0)
         nc.vector.tensor_copy(out=runs(window[:, 0:LATE_CLEAR]), in_=late_seed[:].unsqueeze(1).to_broadcast([P, LATE_CLEAR // SEED, SEED]))
 
-        groups = ((0, 128), (128, 128), (256, 256), (512, 256), (768, 256))
+        groups = ((0, 128), (128, 128), (256, 128), (384, 128), (512, 128), (640, 128), (768, 256))
         accs = {t: psum.tile([P, width], F32, name="acc%d" % t) for t, width in groups}
         widths = dict(groups)
 
@@ -125,8 +128,10 @@ def tile_picked_wroute2_lingelu_l_kernel(tc, x_words, x_scales, gate, w1, dst, o
             width = widths[t]
             if t < EARLY:
                 words = early[g][:, 2 * t:2 * (t + width)]
+            elif t < AHEAD:
+                words = middle[:, g, 2 * (t - EARLY):2 * (t - EARLY + width)]
             else:
-                words = late[:, g, 2 * (t - EARLY):2 * (t - EARLY + width)]
+                words = late[:, g, :]
             nc.tensor.matmul_mx(
                 out=accs[t][:],
                 lhsT=w_code[g][:].bitcast(FP8X4),
@@ -159,17 +164,23 @@ def tile_picked_wroute2_lingelu_l_kernel(tc, x_words, x_scales, gate, w1, dst, o
             else:
                 nc.vector.tensor_tensor(window[:].indirect(places), ys[s][:], gate_of(a, b), MULT)
 
-        for t in (0, 128, 256, 512):
+        for t in (0, 128, 256):
             multiply(t, 0)
-        for t in (0, 128, 256, 512):
+        for t in (0, 128, 256, 384):
+            if t == 384:
+                multiply(t, 0)
+            multiply(t, 1)
+            finish(t)
+        for t in range(EARLY, AHEAD, GROUP):
+            multiply(t, 0)
             multiply(t, 1)
             finish(t)
         scatter(0)
         scatter(1)
-        nc.vector.tensor_tensor(gated[2][:], ys[2][:], gate_of(512, 768), MULT)
-        multiply(EARLY, 0)
-        multiply(EARLY, 1)
-        finish(EARLY)
+        nc.vector.tensor_tensor(gated[2][:], ys[2][:], gate_of(EARLY, AHEAD), MULT)
+        multiply(AHEAD, 0)
+        multiply(AHEAD, 1)
+        finish(AHEAD)
         scatter(2)
         scatter(3)
 

@@ -26,7 +26,7 @@ PIECE = 256
 GROUP = 128
 EARLY = 512
 AHEAD = 768
-GATE_LOADS = ((0, 256), (256, 512), (512, 1024))
+GATE_LOADS = ((0, 256), (256, 768), (768, 1024))
 SEED = 128
 LATE_CLEAR = 512
 CLEAR = 1280
@@ -55,7 +55,7 @@ def tile_picked_wroute2_lingelu_l_kernel(tc, x_words, x_scales, gate, w1, dst, o
         w_raw = [keep.tile([P, PACK, N], F32, name="w_raw%d" % g) for g in range(PASSES)]
         early = [keep.tile([P, 2 * EARLY], U8, name="early%d" % g, align_bytes=64) for g in range(PASSES)]
         middle = keep.tile([P, PASSES, 2 * (AHEAD - EARLY)], U8, name="middle", align_bytes=64)
-        late = keep.tile([P, PASSES, 2 * (T - AHEAD)], U8, name="late", align_bytes=64)
+        late = keep.tile([P, PASSES, 2 * (T - AHEAD)], U8, name="late", tag="late", align_bytes=64)
         x_scale = keep.tile([P, PASSES, T], U8, name="x_scale", align_bytes=64)
         gates = [keep.tile([P, b - a], F32, name="gate%d" % a) for a, b in GATE_LOADS]
 
@@ -89,8 +89,8 @@ def tile_picked_wroute2_lingelu_l_kernel(tc, x_words, x_scales, gate, w1, dst, o
         load_both(middle, EARLY, AHEAD)
         load_gate(0)
         load_gate(1)
-        load_both(late, AHEAD, T)
         nc.sync.dma_start(offsets[:], dst)
+        load_both(late, AHEAD, T)
         for r in range(4):
             load_scales(nc.sync, r, AHEAD, T)
         load_gate(2)
@@ -120,7 +120,7 @@ def tile_picked_wroute2_lingelu_l_kernel(tc, x_words, x_scales, gate, w1, dst, o
         nc.vector.memset(late_seed[:], 0.0)
         nc.vector.tensor_copy(out=runs(window[:, 0:LATE_CLEAR]), in_=late_seed[:].unsqueeze(1).to_broadcast([P, LATE_CLEAR // SEED, SEED]))
 
-        groups = ((0, 128), (128, 128), (256, 128), (384, 128), (512, 128), (640, 128), (768, 256))
+        groups = ((0, 128), (128, 128), (256, 256), (512, 128), (640, 128), (768, 256))
         accs = {t: psum.tile([P, width], F32, name="acc%d" % t) for t, width in groups}
         widths = dict(groups)
 
@@ -147,7 +147,7 @@ def tile_picked_wroute2_lingelu_l_kernel(tc, x_words, x_scales, gate, w1, dst, o
             return gates[i][:, a - GATE_LOADS[i][0]:b - GATE_LOADS[i][0]]
 
         ys = [keep.tile([P, PIECE], F32, name="y%d" % s) for s in range(T // PIECE)]
-        gated = {s: keep.tile([P, PIECE], F32, name="gated%d" % s) for s in (0, 2)}
+        gated = {0: keep.tile([P, PIECE], F32, name="gated0")}
 
         def finish(t):
             width = widths[t]
@@ -159,16 +159,14 @@ def tile_picked_wroute2_lingelu_l_kernel(tc, x_words, x_scales, gate, w1, dst, o
         def scatter(s):
             a, b = s * PIECE, (s + 1) * PIECE
             places = offsets[:, a // 16:b // 16]
-            if s in gated:
+            if s % 2 == 0:
                 nc.scalar.activation(out=side[:].indirect(places), in_=gated[s][:], func=COPY)
             else:
                 nc.vector.tensor_tensor(window[:].indirect(places), ys[s][:], gate_of(a, b), MULT)
 
         for t in (0, 128, 256):
             multiply(t, 0)
-        for t in (0, 128, 256, 384):
-            if t == 384:
-                multiply(t, 0)
+        for t in (0, 128, 256):
             multiply(t, 1)
             finish(t)
         for t in range(EARLY, AHEAD, GROUP):
@@ -177,10 +175,11 @@ def tile_picked_wroute2_lingelu_l_kernel(tc, x_words, x_scales, gate, w1, dst, o
             finish(t)
         scatter(0)
         scatter(1)
-        nc.vector.tensor_tensor(gated[2][:], ys[2][:], gate_of(EARLY, AHEAD), MULT)
         multiply(AHEAD, 0)
         multiply(AHEAD, 1)
         finish(AHEAD)
+        gated[2] = keep.tile([P, PIECE], F32, name="gated2", tag="late", align_bytes=64)
+        nc.vector.tensor_tensor(gated[2][:], ys[2][:], gate_of(EARLY, AHEAD), MULT)
         scatter(2)
         scatter(3)
 

@@ -31,6 +31,7 @@ SEED = 128
 LATE_CLEAR = 512
 CLEAR = 1280
 STORES = (256, 256, 512, 512, 512)
+BURST = 256
 
 
 def tile_picked_wroute2_lingelu_l_kernel(tc, x_words, x_scales, gate, w1, dst, out):
@@ -39,7 +40,7 @@ def tile_picked_wroute2_lingelu_l_kernel(tc, x_words, x_scales, gate, w1, dst, o
         keep = ctx.enter_context(tc.tile_pool(name="keep", bufs=1))
         psum = ctx.enter_context(tc.psum_pool(name="psum", bufs=1))
 
-        offsets = keep.tile([P, T // 16], U16, name="offsets")
+        offsets = keep.tile([P, T // 16], U16, name="offsets", align_bytes=BURST)
         window = keep.tile([P, U], F32, name="window")
         side = keep.tile([P, U], F32, name="side")
         seed = keep.tile([P, SEED], F32, name="seed")
@@ -52,12 +53,12 @@ def tile_picked_wroute2_lingelu_l_kernel(tc, x_words, x_scales, gate, w1, dst, o
         nc.vector.tensor_copy(out=runs(window[:, LATE_CLEAR:]), in_=zeros.to_broadcast([P, (U - LATE_CLEAR) // SEED, SEED]))
         nc.vector.tensor_copy(out=runs(side[:, 0:CLEAR]), in_=zeros.to_broadcast([P, CLEAR // SEED, SEED]))
 
-        w_raw = [keep.tile([P, PACK, N], F32, name="w_raw%d" % g) for g in range(PASSES)]
-        early = [keep.tile([P, 2 * EARLY], U8, name="early%d" % g, align_bytes=64) for g in range(PASSES)]
-        middle = keep.tile([P, PASSES, 2 * (AHEAD - EARLY)], U8, name="middle", align_bytes=64)
-        late = keep.tile([P, PASSES, 2 * (T - AHEAD)], U8, name="late", tag="late", align_bytes=64)
-        x_scale = keep.tile([P, PASSES, T], U8, name="x_scale", align_bytes=64)
-        gates = [keep.tile([P, b - a], F32, name="gate%d" % a) for a, b in GATE_LOADS]
+        w_raw = [keep.tile([P, PACK, N], F32, name="w_raw%d" % g, align_bytes=BURST) for g in range(PASSES)]
+        early = [keep.tile([P, 2 * EARLY], U8, name="early%d" % g, align_bytes=BURST) for g in range(PASSES)]
+        middle = keep.tile([P, PASSES, 2 * (AHEAD - EARLY)], U8, name="middle", align_bytes=BURST)
+        late = keep.tile([P, PASSES, 2 * (T - AHEAD)], U8, name="late", tag="late", align_bytes=BURST)
+        x_scale = keep.tile([P, PASSES, T], U8, name="x_scale", align_bytes=BURST)
+        gates = [keep.tile([P, b - a], F32, name="gate%d" % a, align_bytes=BURST) for a, b in GATE_LOADS]
 
         def load_weights(g):
             nc.sync.dma_start(out=w_raw[g][:], in_=w1[g * K_PASS:(g + 1) * K_PASS, :].rearrange("(p j) m -> p j m", j=PACK))
@@ -178,14 +179,14 @@ def tile_picked_wroute2_lingelu_l_kernel(tc, x_words, x_scales, gate, w1, dst, o
         multiply(AHEAD, 0)
         multiply(AHEAD, 1)
         finish(AHEAD)
-        gated[2] = keep.tile([P, PIECE], F32, name="gated2", tag="late", align_bytes=64)
+        gated[2] = keep.tile([P, PIECE], F32, name="gated2", tag="late", align_bytes=BURST)
         nc.vector.tensor_tensor(gated[2][:], ys[2][:], gate_of(EARLY, AHEAD), MULT)
         scatter(2)
         scatter(3)
 
         a = 0
         for width in STORES:
-            total = keep.tile([P, width], F32, name="total%d" % a)
+            total = keep.tile([P, width], F32, name="total%d" % a, align_bytes=BURST)
             nc.vector.tensor_tensor(total[:], window[:, a:a + width], side[:, a:a + width], ADD)
             nc.sync.dma_start(out=out[:, a:a + width], in_=total[:])
             a += width

from contextlib import ExitStack

import concourse.mybir as mybir

K, T, N, U = 1024, 1024, 128, 2048
FLOPS = 2 * K * T * N

F32 = mybir.dt.float32
BF16 = mybir.dt.bfloat16
I32 = mybir.dt.int32
U32 = mybir.dt.uint32
U16 = mybir.dt.uint16
U8 = mybir.dt.uint8
FP8X4 = mybir.dt.float8_e4m3fn_x4
FP4X4 = mybir.dt.float4_e2m1fn_x4
GELU = mybir.ActivationFunctionType.Gelu_apprx_tanh
COPY = mybir.ActivationFunctionType.Copy
MULT = mybir.AluOpType.mult
ADD = mybir.AluOpType.add

P = 128
PACK = 4
K_PASS = P * PACK
PASSES = K // K_PASS
PIECE = 256
GROUP = 128
EARLY = 512
AHEAD = 768
GATE_LOADS = ((0, 256), (256, 768), (768, 1024))
SEED = 128
LATE_CLEAR = 512
CLEAR = 1280
STORES = (256, 256, 512, 512, 512)
BURST = 256


def tile_picked_wroute2_lingelu_l_kernel(tc, x_words, x_scales, gate, w1, dst, out):
    nc = tc.nc
    with ExitStack() as ctx:
        keep = ctx.enter_context(tc.tile_pool(name="keep", bufs=1))
        psum = ctx.enter_context(tc.psum_pool(name="psum", bufs=1))

        offsets = keep.tile([P, T // 16], U16, name="offsets", align_bytes=BURST)
        window = keep.tile([P, U], F32, name="window")
        side = keep.tile([P, U], F32, name="side")
        seed = keep.tile([P, SEED], F32, name="seed")
        nc.vector.memset(seed[:], 0.0)
        zeros = seed[:].unsqueeze(1)

        def runs(ap):
            return ap.rearrange("p (r c) -> p r c", c=SEED)

        nc.vector.tensor_copy(out=runs(window[:, LATE_CLEAR:]), in_=zeros.to_broadcast([P, (U - LATE_CLEAR) // SEED, SEED]))
        nc.vector.tensor_copy(out=runs(side[:, 0:CLEAR]), in_=zeros.to_broadcast([P, CLEAR // SEED, SEED]))

        w_raw = [keep.tile([P, PACK, N], F32, name="w_raw%d" % g, align_bytes=BURST) for g in range(PASSES)]
        early = [keep.tile([P, 2 * EARLY], U8, name="early%d" % g, align_bytes=BURST) for g in range(PASSES)]
        middle = keep.tile([P, PASSES, 2 * (AHEAD - EARLY)], U8, name="middle", align_bytes=BURST)
        late = keep.tile([P, PASSES, 2 * (T - AHEAD)], U8, name="late", tag="late", align_bytes=BURST)
        x_scale = keep.tile([P, PASSES, T], U8, name="x_scale", align_bytes=BURST)
        gates = [keep.tile([P, b - a], F32, name="gate%d" % a, align_bytes=BURST) for a, b in GATE_LOADS]

        def load_weights(g):
            nc.sync.dma_start(out=w_raw[g][:], in_=w1[g * K_PASS:(g + 1) * K_PASS, :].rearrange("(p j) m -> p j m", j=PACK))

        def load_early(g):
            nc.sync.dma_start(out=early[g][:].bitcast(I32), in_=x_words[g, :, 0:2 * EARLY].bitcast(I32))

        def load_both(tile, a, b):
            nc.sync.dma_start(out=tile[:].bitcast(I32), in_=x_words[:, :, 2 * a:2 * b].rearrange("z p b -> p z b").bitcast(I32))

        def load_scales(engine, r, a, b):
            engine.dma_start(
                out=x_scale[r:P:32, :, a:b].bitcast(I32),
                in_=x_scales[:, r:16:4, a:b].rearrange("z q c -> q z c").bitcast(I32),
            )

        def load_gate(i):
            a, b = GATE_LOADS[i]
            nc.sync.dma_start(out=gates[i][:], in_=gate[:, a:b])

        load_scales(nc.scalar, 0, 0, AHEAD)
        load_scales(nc.scalar, 1, 0, AHEAD)
        load_weights(0)
        load_weights(1)
        load_scales(nc.sync, 2, 0, AHEAD)
        load_scales(nc.sync, 3, 0, AHEAD)
        load_early(0)
        load_early(1)
        load_both(middle, EARLY, AHEAD)
        load_gate(0)
        load_gate(1)
        nc.sync.dma_start(offsets[:], dst)
        load_both(late, AHEAD, T)
        for r in range(4):
            load_scales(nc.sync, r, AHEAD, T)
        load_gate(2)

        nc.scalar.activation(out=runs(side[:, CLEAR:]), in_=zeros.to_broadcast([P, (U - CLEAR) // SEED, SEED]), func=GELU)

        w_code = []
        w_scale = []
        for g in range(PASSES):
            grouped = keep.tile([P, N, PACK], BF16, name="grouped%d" % g, tag="pass%d" % g, align_bytes=64)
            codes = keep.tile([P, N], U32, name="w_code%d" % g, align_bytes=64)
            scales = keep.tile([P, N], U8, name="w_scale%d" % g, align_bytes=64)
            halves = [slice(0, N // 2), slice(N // 2, N)]
            for cols in halves:
                nc.vector.tensor_copy(
                    out=grouped[:, cols, :].rearrange("p (c i) t -> p c t i", i=4),
                    in_=w_raw[g][:, :, cols].rearrange("p t (c i) -> p c t i", i=4),
                )
            for cols in halves:
                nc.vector.quantize_mx(
                    out=codes[:, cols].bitcast(FP8X4), scales=scales[:, cols], in_=grouped[:, cols, :].rearrange("p m t -> p (m t)")
                )
            w_code.append(codes)
            w_scale.append(scales)

        late_seed = keep.tile([P, SEED], F32, name="late_seed", tag="pass1", align_bytes=64)
        nc.vector.memset(late_seed[:], 0.0)
        nc.vector.tensor_copy(out=runs(window[:, 0:LATE_CLEAR]), in_=late_seed[:].unsqueeze(1).to_broadcast([P, LATE_CLEAR // SEED, SEED]))

        groups = ((0, 128), (128, 128), (256, 256), (512, 128), (640, 128), (768, 256))
        accs = {t: psum.tile([P, width], F32, name="acc%d" % t) for t, width in groups}
        widths = dict(groups)

        def multiply(t, g):
            width = widths[t]
            if t < EARLY:
                words = early[g][:, 2 * t:2 * (t + width)]
            elif t < AHEAD:
                words = middle[:, g, 2 * (t - EARLY):2 * (t - EARLY + width)]
            else:
                words = late[:, g, :]
            nc.tensor.matmul_mx(
                out=accs[t][:],
                lhsT=w_code[g][:].bitcast(FP8X4),
                lhsT_scale=w_scale[g][:],
                rhs=words.bitcast(FP4X4),
                rhs_scale=x_scale[:, g, t:t + width],
                start=(g == 0),
                stop=(g == PASSES - 1),
            )

        def gate_of(a, b):
            i = [k for k, (lo, hi) in enumerate(GATE_LOADS) if lo <= a < hi][0]
            return gates[i][:, a - GATE_LOADS[i][0]:b - GATE_LOADS[i][0]]

        ys = [keep.tile([P, PIECE], F32, name="y%d" % s) for s in range(T // PIECE)]
        gated = {0: keep.tile([P, PIECE], F32, name="gated0")}

        def finish(t):
            width = widths[t]
            s, c = divmod(t, PIECE)
            nc.scalar.activation(out=ys[s][:, c:c + width], in_=accs[t][:], func=GELU)
            if s == 0:
                nc.vector.tensor_tensor(gated[s][:, c:c + width], ys[s][:, c:c + width], gate_of(t, t + width), MULT)

        def scatter(s):
            a, b = s * PIECE, (s + 1) * PIECE
            places = offsets[:, a // 16:b // 16]
            if s % 2 == 0:
                nc.scalar.activation(out=side[:].indirect(places), in_=gated[s][:], func=COPY)
            else:
                nc.vector.tensor_tensor(window[:].indirect(places), ys[s][:], gate_of(a, b), MULT)

        for t in (0, 128, 256):
            multiply(t, 0)
        for t in (0, 128, 256):
            multiply(t, 1)
            finish(t)
        for t in range(EARLY, AHEAD, GROUP):
            multiply(t, 0)
            multiply(t, 1)
            finish(t)
        scatter(0)
        scatter(1)
        multiply(AHEAD, 0)
        multiply(AHEAD, 1)
        finish(AHEAD)
        gated[2] = keep.tile([P, PIECE], F32, name="gated2", tag="late", align_bytes=BURST)
        nc.vector.tensor_tensor(gated[2][:], ys[2][:], gate_of(EARLY, AHEAD), MULT)
        scatter(2)
        scatter(3)

        a = 0
        for width in STORES:
            total = keep.tile([P, width], F32, name="total%d" % a, align_bytes=BURST)
            nc.vector.tensor_tensor(total[:], window[:, a:a + width], side[:, a:a + width], ADD)
            nc.sync.dma_start(out=out[:, a:a + width], in_=total[:])
            a += width
